import numpy as np
import ml_dtypes


def mxq(x, axis, fmt="e4m3"):
    dtype, down = {"e4m3": (ml_dtypes.float8_e4m3fn, 7), "e5m2": (ml_dtypes.float8_e5m2, 14)}[fmt]
    v = np.moveaxis(np.asarray(x, np.float32).astype(ml_dtypes.bfloat16).astype(np.float64), axis, -1)
    blocks = v.reshape(v.shape[:-1] + (-1, 32))
    amax = np.abs(blocks).max(-1, keepdims=True)
    byte = np.maximum(np.where(amax > 0, np.frexp(amax)[1] - 1 + 127, 0) - down, 1)
    scale = np.exp2(byte - 127.0)
    codes = (blocks / scale).astype(np.float32).astype(dtype).astype(np.float64)
    return np.moveaxis((codes * scale).reshape(v.shape), -1, axis)


WIDE = False


def mx_kscale(k):
    if not WIDE:
        return np.ones(k)
    levels = np.array([10, -10, 5, -5, 0])
    if k % 512:
        return np.exp2(np.random.permutation(np.resize(levels, k // 32))).repeat(32)
    a = np.empty((k // 512, 16))
    for p in range(k // 512):
        a[p, :8] = np.random.permutation(np.resize(levels, 8))
        for g in range(8):
            far = levels[np.abs(levels - a[p, g]) >= 10]
            a[p, g + 8] = far[np.random.randint(len(far))]
    return np.exp2(a.ravel()).repeat(32)


def f64(x):
    return np.asarray(x).astype(np.float64)


def striped(idx):
    return np.tile(idx.reshape(-1, 16).T, (8, 1)).astype(np.uint16)


def unstriped(offs):
    return offs[:16].T.reshape(-1).astype(np.int64)


def striped8(idx):
    return np.concatenate([x.reshape(-1, 16).T for x in idx]).astype(np.uint16)


def runs(offs, k):
    lists = np.stack([offs[16 * r : 16 * r + 16].T.reshape(-1) for r in range(8)]).astype(np.int64)
    return lists[np.arange(k) % 512 // 64]


def pack_weight(w):
    k, n = w.shape
    w = f64(np.asarray(w, np.float32).astype(ml_dtypes.bfloat16)).reshape(k // 32, 32, n)
    amax = np.abs(w).max(1)
    byte = np.clip(np.where(amax > 0, np.frexp(amax)[1] - 1 + 127 - 7, 1), 1, 254)
    scaled = (w * np.exp2(127.0 - byte)[:, None, :]).reshape(k, n).astype(np.float32)
    words = np.ascontiguousarray(scaled.reshape(k // 512, 128, 4, n).transpose(0, 1, 3, 2)).astype(ml_dtypes.float8_e4m3fn).view(np.uint8)
    return words, np.ascontiguousarray(byte.astype(np.uint8).reshape(k // 512, 16, n))


def unpack_weight(words, scales):
    g, p, n, _ = words.shape
    vals = np.ascontiguousarray(words).view(ml_dtypes.float8_e4m3fn).astype(np.float64) * np.repeat(np.exp2(scales.astype(np.float64) - 127.0), 8, axis=1)[..., None]
    return vals.transpose(0, 1, 3, 2).reshape(g * 512, n)


K, T, S, N, H, J = 512, 2048, 512, 512, 512, 512


def setup_inputs():
    n = np.random.standard_normal
    s = mx_kscale(K)[:, None]
    u = mx_kscale(S)
    packed_xT = pack_weight(n((K, T)) * s)
    return {
        "x_words": packed_xT[0],
        "x_scales": packed_xT[1],
        "wa": (n((K, H)) / np.sqrt(K) / s).astype(np.float32),
        "gt": (np.random.uniform(0.5, 1.5, (S, 1)) * u[:, None]).astype(np.float32),
        "w1": (n((S, N)) / np.sqrt(S) / u[:, None]).astype(np.float32),
        "tab": n((N, J)).astype(np.float32),
        "offs": striped(np.random.permutation(T)[:S]),
        "n1": striped8(np.stack([np.random.permutation(H) for _ in range(8)])),
        "n2": striped8(np.stack([np.random.permutation(H) for _ in range(8)])),
        "n3": striped8(np.random.randint(0, J, (8, H))),
        "n4": striped8(np.stack([np.random.permutation(H) for _ in range(8)])),
    }


def reference(x_words, x_scales, wa, gt, w1, tab, offs, n1, n2, n3, n4):
    xq = unpack_weight(x_words, x_scales)[:, unstriped(offs)]
    y = xq.T @ mxq(f64(wa), 0, "e4m3")
    z = f64(gt) * ((np.tanh(y[np.arange(S)[:, None], runs(n1, S)] - y)) * (y[np.arange(S)[:, None], runs(n2, S)]))
    h = mxq(f64(w1), 0, "e4m3").T @ mxq(z, 0, "e4m3")
    return np.maximum(h + f64(tab)[np.arange(N)[:, None], runs(n3, N)], h[np.arange(N)[:, None], runs(n4, N)])

@@ -1,0 +1,240 @@
+from contextlib import ExitStack
+
+import concourse.mybir as mybir
+
+F32 = mybir.dt.float32
+BF16 = mybir.dt.bfloat16
+I32 = mybir.dt.int32
+U32 = mybir.dt.uint32
+U16 = mybir.dt.uint16
+U8 = mybir.dt.uint8
+FP8X4 = mybir.dt.float8_e4m3fn_x4
+ALU = mybir.AluOpType
+ACT = mybir.ActivationFunctionType
+
+P = 128
+PACK = 4
+T = 2048
+S = 512
+H = 512
+HALF = H // 2
+LIST_HALF = HALF // 16
+WA_SCALAR_COLS = 96
+
+FLOPS = 2 * 2 * 512 * 512 * 512
+
+
+def half(a):
+    return slice(a * HALF, (a + 1) * HALF)
+
+
+def list_half(lst, a):
+    return lst[:, a * LIST_HALF : (a + 1) * LIST_HALF]
+
+
+def interleave(copy, dst, src):
+    copy(
+        out=dst.rearrange("p (c i j) -> p c j i", i=4, j=PACK),
+        in_=src.rearrange("p j (c i) -> p c j i", i=4),
+    )
+
+
+def tile_picked_tokfdifkind_none_p_kernel(
+    tc, x_words, x_scales, wa, gt, w1, tab, offs, n1, n2, n3, n4, out
+):
+    nc = tc.nc
+    with ExitStack() as ctx:
+        lists = ctx.enter_context(tc.tile_pool(name="lists", bufs=1))
+        sb = ctx.enter_context(tc.tile_pool(name="sb", bufs=1))
+        ps = ctx.enter_context(tc.psum_pool(name="ps", bufs=1))
+
+        def load_list(src, name):
+            lst = lists.tile([P, S // 16], U16, name=name)
+            nc.sync.dma_start(lst[:], src)
+            return lst
+
+        def dealt(rows, t):
+            return rows.rearrange("(q t e) n -> t q e n", t=PACK, e=8)[t]
+
+        wa_rows = wa.rearrange("(p j) n -> p j n", j=PACK)
+
+        xs = sb.tile([P, T], U8, name="xs", align_bytes=64)
+        nc.vector.memset(xs[:].bitcast(I32), 0)
+        warm = sb.tile([P, 1], F32, name="warm")
+        nc.gpsimd.memset(warm[:], 0.0)
+        warm_out = sb.tile([P, 1], F32, name="warm_out")
+        nc.scalar.activation(out=warm_out[:], in_=warm[:], func=ACT.Tanh)
+
+        offs_l = load_list(offs, "offs_l")
+        wa_raw = [sb.tile([P, PACK, HALF], F32, name="wa_raw%d" % a, tag="wa_raw%d" % a) for a in range(2)]
+        nc.sync.dma_start(out=wa_raw[0][:], in_=wa_rows[:, :, half(0)])
+        n1_l = load_list(n1, "n1_l")
+        for q in range(4):
+            nc.sync.dma_start(
+                out=xs[32 * q : 32 * q + 4, :].bitcast(I32),
+                in_=x_scales[0, 4 * q : 4 * q + 4, :].bitcast(I32),
+            )
+        xw = sb.tile([P, T], I32, name="xw", align_bytes=64)
+        nc.sync.dma_start(out=xw[:], in_=x_words[0].rearrange("p n t -> p (n t)").bitcast(I32))
+        nc.sync.dma_start(out=wa_raw[1][:], in_=wa_rows[:, :, half(1)])
+
+        tab_sb = [sb.tile([P, H], F32, name="tab%d" % t) for t in range(PACK)]
+        gt_sb = [sb.tile([P, 1], F32, name="gt%d" % t) for t in range(PACK)]
+        w1_raw = sb.tile([P, PACK, H], F32, name="w1_raw")
+        nc.sync.dma_start(out=tab_sb[0][:], in_=dealt(tab, 0))
+        nc.sync.dma_start(out=gt_sb[0][:], in_=dealt(gt, 0))
+        n3_l = load_list(n3, "n3_l")
+        n2_l = load_list(n2, "n2_l")
+        for t in range(1, PACK):
+            nc.sync.dma_start(out=gt_sb[t][:], in_=dealt(gt, t))
+        for j in range(PACK):
+            nc.sync.dma_start(out=w1_raw[:, j, :], in_=dealt(w1, j))
+        for t in range(1, PACK):
+            nc.sync.dma_start(out=tab_sb[t][:], in_=dealt(tab, t))
+        n4_l = load_list(n4, "n4_l")
+
+        xs_g = sb.tile([P, S], U8, name="xs_g", align_bytes=64)
+        nc.vector.tensor_copy(out=xs_g[:], in_=xs[:].indirect(offs_l[:]))
+        wa_bf = [sb.tile([P, HALF * PACK], BF16, name="wa_bf%d" % a, tag="wa_bf%d" % a, align_bytes=64) for a in range(2)]
+        wa_q = [sb.tile([P, HALF], U32, name="wa_q%d" % a, align_bytes=64) for a in range(2)]
+        wa_s = [sb.tile([P, HALF], U8, name="wa_s%d" % a, align_bytes=64) for a in range(2)]
+        interleave(nc.scalar.copy, wa_bf[0][:], wa_raw[0][:])
+        nc.vector.quantize_mx(out=wa_q[0][:].bitcast(FP8X4), scales=wa_s[0][:], in_=wa_bf[0][:])
+        xs_d = sb.tile([P, S], U8, name="xs_d", align_bytes=64)
+        nc.vector.tensor_copy(
+            out=xs_d[:].bitcast(I32).rearrange("p (t q w) -> p t q w", t=PACK, w=2),
+            in_=xs_g[:].bitcast(I32).rearrange("p (q t w) -> p t q w", t=PACK, w=2),
+        )
+        xw_d = sb.tile([P, S], U32, name="xw_d", align_bytes=64)
+        nc.vector.tensor_copy(
+            out=xw_d[:].rearrange("p (t q e) -> p q t e", t=PACK, e=8),
+            in_=xw[:].bitcast(U32).indirect(offs_l[:]),
+        )
+        c = WA_SCALAR_COLS
+        interleave(nc.scalar.copy, wa_bf[1][:, : c * PACK], wa_raw[1][:, :, :c])
+        interleave(nc.vector.tensor_copy, wa_bf[1][:, c * PACK :], wa_raw[1][:, :, c:])
+        nc.vector.quantize_mx(out=wa_q[1][:].bitcast(FP8X4), scales=wa_s[1][:], in_=wa_bf[1][:])
+
+        def banks(first_tag, name):
+            lone = [ps.tile([P, HALF], F32, name="%s0%d" % (name, a), tag="bank%d" % ((first_tag + a) % 8)) for a in range(2)]
+            whole = [ps.tile([P, H], F32, name="%s%d" % (name, t), tag="bank%d" % ((first_tag + 1 + t) % 8)) for t in range(1, PACK)]
+            return lone, whole
+
+        def part(bk, t, a):
+            return bk[0][a][:] if t == 0 else bk[1][t - 1][:, half(a)]
+
+        def tile_cols(t):
+            return slice(t * P, (t + 1) * P)
+
+        y_ps = banks(0, "y")
+        for a in range(2):
+            for t in range(PACK):
+                nc.tensor.matmul_mx(
+                    out=part(y_ps, t, a),
+                    lhsT=xw_d[:, tile_cols(t)].bitcast(FP8X4),
+                    lhsT_scale=xs_d[:, tile_cols(t)],
+                    rhs=wa_q[a][:].bitcast(FP8X4),
+                    rhs_scale=wa_s[a][:],
+                    start=True,
+                    stop=True,
+                )
+
+        def fetch_tab(t, tag):
+            got = sb.tile([P, H], F32, name="tab_g%d" % t, tag=tag, align_bytes=64)
+            for a in range(2):
+                nc.vector.tensor_copy(out=got[:, half(a)], in_=tab_sb[t][:].indirect(list_half(n3_l, a)))
+            return got
+
+        tab_g = [fetch_tab(0, "wa_bf1")]
+
+        prod = [sb.tile([P, PACK, HALF], F32, name="prod%d" % a) for a in range(2)]
+        for t in range(PACK):
+            y_win = sb.tile([P, H], F32, name="y_win%d" % t, tag="wa_raw1" if t == 0 else "y_win%d" % t)
+            y_own = [sb.tile([P, HALF], F32, name="y_own%d%d" % (t, a)) for a in range(2)]
+            gy_win = sb.tile([P, H], F32, name="gy_win%d" % t)
+            if t == 0:
+                nc.scalar.copy(out=y_win[:, half(0)], in_=part(y_ps, 0, 0))
+                nc.scalar.copy(out=y_own[0][:], in_=y_win[:, half(0)])
+                nc.scalar.activation(out=gy_win[:, half(0)], in_=y_win[:, half(0)], func=ACT.Copy, scale=gt_sb[0][:])
+                nc.scalar.copy(out=y_win[:, half(1)], in_=part(y_ps, 0, 1))
+                nc.scalar.copy(out=y_own[1][:], in_=part(y_ps, 0, 1))
+            else:
+                nc.scalar.copy(out=y_win[:], in_=y_ps[1][t - 1][:])
+                for a in range(2):
+                    nc.scalar.copy(out=y_own[a][:], in_=part(y_ps, t, a))
+            diff = [sb.tile([P, HALF], F32, name="diff%d%d" % (t, a)) for a in range(2)]
+            th = [sb.tile([P, HALF], F32, name="th%d%d" % (t, a), tag="th%d%d" % (t, a), align_bytes=64) for a in range(2)]
+            for a in range(2):
+                nc.vector.tensor_tensor(diff[a][:], y_win[:].indirect(list_half(n1_l, a)), y_own[a][:], ALU.subtract)
+            if t == 0:
+                nc.scalar.activation(out=gy_win[:, half(1)], in_=part(y_ps, 0, 1), func=ACT.Copy, scale=gt_sb[0][:])
+            else:
+                nc.scalar.activation(out=gy_win[:], in_=y_ps[1][t - 1][:], func=ACT.Copy, scale=gt_sb[t][:])
+            for a in range(2):
+                nc.scalar.activation(out=th[a][:], in_=diff[a][:], func=ACT.Tanh)
+            for a in range(2):
+                nc.vector.tensor_tensor(prod[a][:, t, :], gy_win[:].indirect(list_half(n2_l, a)), th[a][:], ALU.mult)
+
+        z_bf = [sb.tile([P, HALF * PACK], BF16, name="z_bf%d" % a, tag="z_bf%d" % a, align_bytes=64) for a in range(2)]
+        z_q = [sb.tile([P, HALF], U32, name="z_q%d" % a, align_bytes=64) for a in range(2)]
+        z_s = [sb.tile([P, HALF], U8, name="z_s%d" % a, align_bytes=64) for a in range(2)]
+        w1_q = [sb.tile([P, P], U32, name="w1_q%d" % t, align_bytes=64) for t in range(PACK)]
+        w1_s = [sb.tile([P, P], U8, name="w1_s%d" % t, align_bytes=64) for t in range(PACK)]
+        w1_bf = [sb.tile([P, P * PACK], BF16, name="w1_bf%d" % t, align_bytes=64) for t in range(PACK)]
+
+        def cast_w1(t):
+            nc.scalar.copy(
+                out=w1_bf[t][:].rearrange("p (q u i j) -> p q u j i", u=2, i=4, j=PACK),
+                in_=w1_raw[:].rearrange("p j (q t u i) -> p t q u j i", t=PACK, u=2, i=4)[:, t],
+            )
+
+        def quantize_w1(t):
+            nc.vector.quantize_mx(out=w1_q[t][:].bitcast(FP8X4), scales=w1_s[t][:], in_=w1_bf[t][:])
+
+        h_ps = banks(5, "h")
+        h_win = [sb.tile([P, H], F32, name="h_win%d" % t) for t in range(PACK)]
+
+        def second_product(t, a):
+            nc.tensor.matmul_mx(
+                out=part(h_ps, t, a),
+                lhsT=w1_q[t][:].bitcast(FP8X4),
+                lhsT_scale=w1_s[t][:],
+                rhs=z_q[a][:].bitcast(FP8X4),
+                rhs_scale=z_s[a][:],
+                start=True,
+                stop=True,
+            )
+
+        for a in range(2):
+            cast_w1(a)
+            interleave(nc.scalar.copy, z_bf[a][:], prod[a][:])
+        tab_g.append(fetch_tab(1, "th31"))
+        for a in range(2):
+            quantize_w1(a)
+            nc.vector.quantize_mx(out=z_q[a][:].bitcast(FP8X4), scales=z_s[a][:], in_=z_bf[a][:])
+            tab_g.append(fetch_tab(2 + a, "z_bf%d" % a))
+            second_product(0, a)
+            nc.scalar.copy(out=h_win[0][:, half(a)], in_=part(h_ps, 0, a))
+            cast_w1(2 + a)
+
+        sums, picks = [], []
+        for t in range(PACK):
+            if t > 0:
+                for a in range(2):
+                    second_product(t, a)
+                nc.scalar.copy(out=h_win[t][:], in_=h_ps[1][t - 1][:])
+            if 0 < t + 2 < PACK:
+                quantize_w1(t + 2)
+            total = sb.tile([P, H], F32, name="total%d" % t)
+            nc.gpsimd.tensor_tensor(total[:], h_win[t][:], tab_g[t][:], ALU.add)
+            pick = sb.tile([P, H], F32, name="pick%d" % t)
+            for a in range(2):
+                nc.vector.tensor_copy(out=pick[:, half(a)], in_=h_win[t][:].indirect(list_half(n4_l, a)))
+            sums.append(total)
+            picks.append(pick)
+        for t in range(PACK):
+            pieces = [half(0), half(1)] if t == PACK - 1 else [slice(0, H)]
+            for n, cols in enumerate(pieces):
+                res = sb.tile([P, cols.stop - cols.start], F32, name="res%d%d" % (t, n))
+                nc.vector.tensor_tensor(res[:], sums[t][:, cols], picks[t][:, cols], ALU.max)
+                nc.sync.dma_start(out=dealt(out, t)[:, :, cols], in_=res[:])

@@ -19,7 +19,6 @@ S = 512
 H = 512
 HALF = H // 2
 LIST_HALF = HALF // 16
-WA_SCALAR_COLS = 96
 
 FLOPS = 2 * 2 * 512 * 512 * 512
 
@@ -59,16 +58,20 @@ def tile_picked_tokfdifkind_none_p_kernel(
         wa_rows = wa.rearrange("(p j) n -> p j n", j=PACK)
 
         xs = sb.tile([P, T], U8, name="xs", align_bytes=64)
-        nc.vector.memset(xs[:].bitcast(I32), 0)
+        nc.gpsimd.memset(xs[:].bitcast(I32), 0)
         warm = sb.tile([P, 1], F32, name="warm")
         nc.gpsimd.memset(warm[:], 0.0)
         warm_out = sb.tile([P, 1], F32, name="warm_out")
         nc.scalar.activation(out=warm_out[:], in_=warm[:], func=ACT.Tanh)
+        y_win = [sb.tile([P, 2 * H], F32, name="y_win%d" % t) for t in range(PACK)]
+        tab_win = [sb.tile([P, H], F32, name="tab_win%d" % t) for t in range(PACK)]
+        for win in y_win[:2]:
+            nc.vector.memset(win[:, H:], 0.0)
 
         offs_l = load_list(offs, "offs_l")
         wa_raw = [sb.tile([P, PACK, HALF], F32, name="wa_raw%d" % a, tag="wa_raw%d" % a) for a in range(2)]
         nc.sync.dma_start(out=wa_raw[0][:], in_=wa_rows[:, :, half(0)])
-        n1_l = load_list(n1, "n1_l")
+        n3_l = load_list(n3, "n3_l")
         for q in range(4):
             nc.sync.dma_start(
                 out=xs[32 * q : 32 * q + 4, :].bitcast(I32),
@@ -78,19 +81,19 @@ def tile_picked_tokfdifkind_none_p_kernel(
         nc.sync.dma_start(out=xw[:], in_=x_words[0].rearrange("p n t -> p (n t)").bitcast(I32))
         nc.sync.dma_start(out=wa_raw[1][:], in_=wa_rows[:, :, half(1)])
 
-        tab_sb = [sb.tile([P, H], F32, name="tab%d" % t) for t in range(PACK)]
         gt_sb = [sb.tile([P, 1], F32, name="gt%d" % t) for t in range(PACK)]
         w1_raw = sb.tile([P, PACK, H], F32, name="w1_raw")
-        nc.sync.dma_start(out=tab_sb[0][:], in_=dealt(tab, 0))
         nc.sync.dma_start(out=gt_sb[0][:], in_=dealt(gt, 0))
-        n3_l = load_list(n3, "n3_l")
+        for t in range(2):
+            nc.sync.dma_start(out=tab_win[t][:], in_=dealt(tab, t))
+        n1_l = load_list(n1, "n1_l")
         n2_l = load_list(n2, "n2_l")
         for t in range(1, PACK):
             nc.sync.dma_start(out=gt_sb[t][:], in_=dealt(gt, t))
         for j in range(PACK):
             nc.sync.dma_start(out=w1_raw[:, j, :], in_=dealt(w1, j))
-        for t in range(1, PACK):
-            nc.sync.dma_start(out=tab_sb[t][:], in_=dealt(tab, t))
+        for t in range(2, PACK):
+            nc.sync.dma_start(out=tab_win[t][:], in_=dealt(tab, t))
         n4_l = load_list(n4, "n4_l")
 
         xs_g = sb.tile([P, S], U8, name="xs_g", align_bytes=64)
@@ -110,9 +113,16 @@ def tile_picked_tokfdifkind_none_p_kernel(
             out=xw_d[:].rearrange("p (t q e) -> p q t e", t=PACK, e=8),
             in_=xw[:].bitcast(U32).indirect(offs_l[:]),
         )
-        c = WA_SCALAR_COLS
-        interleave(nc.scalar.copy, wa_bf[1][:, : c * PACK], wa_raw[1][:, :, :c])
-        interleave(nc.vector.tensor_copy, wa_bf[1][:, c * PACK :], wa_raw[1][:, :, c:])
+        h_win = []
+
+        def fetch_tab(t, tag):
+            win = sb.tile([P, 2 * H], F32, name="h_win%d" % t, tag=tag, align_bytes=64)
+            for a in range(2):
+                nc.vector.tensor_copy(out=win[:, H:][:, half(a)], in_=tab_win[t][:].indirect(list_half(n3_l, a)))
+            h_win.append(win)
+
+        interleave(nc.scalar.copy, wa_bf[1][:], wa_raw[1][:])
+        fetch_tab(0, "h_win0")
         nc.vector.quantize_mx(out=wa_q[1][:].bitcast(FP8X4), scales=wa_s[1][:], in_=wa_bf[1][:])
 
         def banks(first_tag, name):
@@ -139,41 +149,46 @@ def tile_picked_tokfdifkind_none_p_kernel(
                     stop=True,
                 )
 
-        def fetch_tab(t, tag):
-            got = sb.tile([P, H], F32, name="tab_g%d" % t, tag=tag, align_bytes=64)
-            for a in range(2):
-                nc.vector.tensor_copy(out=got[:, half(a)], in_=tab_sb[t][:].indirect(list_half(n3_l, a)))
-            return got
+        fetch_tab(1, "wa_bf1")
 
-        tab_g = [fetch_tab(0, "wa_bf1")]
+        gy_win = [sb.tile([P, 2 * H], F32, name="gy_win%d" % t, tag="wa_raw1" if t == 0 else "gy_win%d" % t) for t in range(PACK)]
+        diff = [sb.tile([P, H], F32, name="diff%d" % t) for t in range(PACK)]
+        th = [y_win[2][:, H:], y_win[3][:, H:]]
+        th.extend(sb.tile([P, H], F32, name="th%d" % t, tag="th%d" % t, align_bytes=64)[:] for t in range(2, PACK))
+        prod_whole = sb.tile([P, PACK, H], F32, name="prod_whole")
 
-        prod = [sb.tile([P, PACK, HALF], F32, name="prod%d" % a) for a in range(2)]
-        for t in range(PACK):
-            y_win = sb.tile([P, H], F32, name="y_win%d" % t, tag="wa_raw1" if t == 0 else "y_win%d" % t)
-            y_own = [sb.tile([P, HALF], F32, name="y_own%d%d" % (t, a)) for a in range(2)]
-            gy_win = sb.tile([P, H], F32, name="gy_win%d" % t)
+        def own(t):
+            return gy_win[t][:, H:]
+
+        def differ(t):
             if t == 0:
-                nc.scalar.copy(out=y_win[:, half(0)], in_=part(y_ps, 0, 0))
-                nc.scalar.copy(out=y_own[0][:], in_=y_win[:, half(0)])
-                nc.scalar.activation(out=gy_win[:, half(0)], in_=y_win[:, half(0)], func=ACT.Copy, scale=gt_sb[0][:])
-                nc.scalar.copy(out=y_win[:, half(1)], in_=part(y_ps, 0, 1))
-                nc.scalar.copy(out=y_own[1][:], in_=part(y_ps, 0, 1))
+                nc.scalar.copy(out=own(0)[:, half(0)], in_=part(y_ps, 0, 0))
+                nc.scalar.copy(out=y_win[0][:, half(0)], in_=own(0)[:, half(0)])
+                nc.scalar.activation(out=gy_win[0][:, half(0)], in_=own(0)[:, half(0)], func=ACT.Copy, scale=gt_sb[0][:])
+                nc.scalar.copy(out=y_win[0][:, half(1)], in_=part(y_ps, 0, 1))
+                nc.scalar.copy(out=own(0)[:, half(1)], in_=part(y_ps, 0, 1))
             else:
-                nc.scalar.copy(out=y_win[:], in_=y_ps[1][t - 1][:])
+                nc.scalar.copy(out=y_win[t][:, :H], in_=y_ps[1][t - 1][:])
+                nc.scalar.copy(out=own(t), in_=y_ps[1][t - 1][:])
+            nc.vector.tensor_tensor(diff[t][:], y_win[t][:].indirect(n1_l[:]), own(t), ALU.subtract)
+
+        def weigh(t):
+            if t == 0:
+                nc.scalar.activation(out=gy_win[0][:, half(1)], in_=part(y_ps, 0, 1), func=ACT.Copy, scale=gt_sb[0][:])
+            else:
+                nc.scalar.activation(out=gy_win[t][:, :H], in_=y_ps[1][t - 1][:], func=ACT.Copy, scale=gt_sb[t][:])
+            nc.scalar.activation(out=th[t], in_=diff[t][:], func=ACT.Tanh)
+            if t < PACK - 1:
+                nc.vector.tensor_tensor(prod_whole[:, t, :], gy_win[t][:].indirect(n2_l[:]), th[t], ALU.mult)
+            else:
                 for a in range(2):
-                    nc.scalar.copy(out=y_own[a][:], in_=part(y_ps, t, a))
-            diff = [sb.tile([P, HALF], F32, name="diff%d%d" % (t, a)) for a in range(2)]
-            th = [sb.tile([P, HALF], F32, name="th%d%d" % (t, a), tag="th%d%d" % (t, a), align_bytes=64) for a in range(2)]
-            for a in range(2):
-                nc.vector.tensor_tensor(diff[a][:], y_win[:].indirect(list_half(n1_l, a)), y_own[a][:], ALU.subtract)
-            if t == 0:
-                nc.scalar.activation(out=gy_win[:, half(1)], in_=part(y_ps, 0, 1), func=ACT.Copy, scale=gt_sb[0][:])
-            else:
-                nc.scalar.activation(out=gy_win[:], in_=y_ps[1][t - 1][:], func=ACT.Copy, scale=gt_sb[t][:])
-            for a in range(2):
-                nc.scalar.activation(out=th[a][:], in_=diff[a][:], func=ACT.Tanh)
-            for a in range(2):
-                nc.vector.tensor_tensor(prod[a][:, t, :], gy_win[:].indirect(list_half(n2_l, a)), th[a][:], ALU.mult)
+                    nc.vector.tensor_tensor(prod_whole[:, t, half(a)], gy_win[t][:].indirect(list_half(n2_l, a)), th[t][:, half(a)], ALU.mult)
+
+        differ(0)
+        for t in range(PACK):
+            if t + 1 < PACK:
+                differ(t + 1)
+            weigh(t)
 
         z_bf = [sb.tile([P, HALF * PACK], BF16, name="z_bf%d" % a, tag="z_bf%d" % a, align_bytes=64) for a in range(2)]
         z_q = [sb.tile([P, HALF], U32, name="z_q%d" % a, align_bytes=64) for a in range(2)]
@@ -192,7 +207,6 @@ def tile_picked_tokfdifkind_none_p_kernel(
             nc.vector.quantize_mx(out=w1_q[t][:].bitcast(FP8X4), scales=w1_s[t][:], in_=w1_bf[t][:])
 
         h_ps = banks(5, "h")
-        h_win = [sb.tile([P, H], F32, name="h_win%d" % t) for t in range(PACK)]
 
         def second_product(t, a):
             nc.tensor.matmul_mx(
@@ -205,36 +219,41 @@ def tile_picked_tokfdifkind_none_p_kernel(
                 stop=True,
             )
 
+        cast_w1(0)
         for a in range(2):
-            cast_w1(a)
-            interleave(nc.scalar.copy, z_bf[a][:], prod[a][:])
-        tab_g.append(fetch_tab(1, "th31"))
+            interleave(nc.scalar.copy, z_bf[a][:], prod_whole[:, :, half(a)])
+        cast_w1(1)
+        cast_w1(2)
+        fetch_tab(2, "th3")
+        quantize_w1(0)
         for a in range(2):
-            quantize_w1(a)
             nc.vector.quantize_mx(out=z_q[a][:].bitcast(FP8X4), scales=z_s[a][:], in_=z_bf[a][:])
-            tab_g.append(fetch_tab(2 + a, "z_bf%d" % a))
+        fetch_tab(3, "z_bf1")
+        quantize_w1(1)
+        quantize_w1(2)
+        for a in range(2):
             second_product(0, a)
             nc.scalar.copy(out=h_win[0][:, half(a)], in_=part(h_ps, 0, a))
-            cast_w1(2 + a)
 
         sums, picks = [], []
         for t in range(PACK):
             if t > 0:
                 for a in range(2):
                     second_product(t, a)
-                nc.scalar.copy(out=h_win[t][:], in_=h_ps[1][t - 1][:])
-            if 0 < t + 2 < PACK:
-                quantize_w1(t + 2)
+                nc.scalar.copy(out=h_win[t][:, :H], in_=h_ps[1][t - 1][:])
+            if t == 1:
+                cast_w1(3)
+                quantize_w1(3)
             total = sb.tile([P, H], F32, name="total%d" % t)
-            nc.gpsimd.tensor_tensor(total[:], h_win[t][:], tab_g[t][:], ALU.add)
             pick = sb.tile([P, H], F32, name="pick%d" % t)
-            for a in range(2):
-                nc.vector.tensor_copy(out=pick[:, half(a)], in_=h_win[t][:].indirect(list_half(n4_l, a)))
+            nc.vector.tensor_copy(out=pick[:], in_=h_win[t][:].indirect(n4_l[:]))
+            nc.gpsimd.tensor_tensor(total[:], h_win[t][:, :H], h_win[t][:, H:], ALU.add)
             sums.append(total)
             picks.append(pick)
+        res = sb.tile([P, PACK * H], F32, name="res", tag="z_bf1", align_bytes=64)
         for t in range(PACK):
-            pieces = [half(0), half(1)] if t == PACK - 1 else [slice(0, H)]
-            for n, cols in enumerate(pieces):
-                res = sb.tile([P, cols.stop - cols.start], F32, name="res%d%d" % (t, n))
-                nc.vector.tensor_tensor(res[:], sums[t][:, cols], picks[t][:, cols], ALU.max)
-                nc.sync.dma_start(out=dealt(out, t)[:, :, cols], in_=res[:])
+            pieces = [slice(0, 384), slice(384, H)] if t == PACK - 1 else [slice(0, H)]
+            for cols in pieces:
+                piece = res[:, t * H : (t + 1) * H][:, cols]
+                nc.vector.tensor_tensor(piece, sums[t][:, cols], picks[t][:, cols], ALU.max)
+                nc.sync.dma_start(out=dealt(out, t)[:, :, cols], in_=piece)

@@ -59,14 +59,10 @@ def tile_picked_tokfdifkind_none_p_kernel(
 
         xs = sb.tile([P, T], U8, name="xs", align_bytes=64)
         nc.gpsimd.memset(xs[:].bitcast(I32), 0)
-        warm = sb.tile([P, 1], F32, name="warm")
-        nc.gpsimd.memset(warm[:], 0.0)
-        warm_out = sb.tile([P, 1], F32, name="warm_out")
-        nc.scalar.activation(out=warm_out[:], in_=warm[:], func=ACT.Tanh)
         y_win = [sb.tile([P, 2 * H], F32, name="y_win%d" % t) for t in range(PACK)]
         tab_win = [sb.tile([P, H], F32, name="tab_win%d" % t) for t in range(PACK)]
-        for win in y_win[:2]:
-            nc.vector.memset(win[:, H:], 0.0)
+        nc.vector.memset(y_win[0][:, H:], 0.0)
+        nc.scalar.activation(out=y_win[1][:, H:], in_=y_win[0][:, H:], func=ACT.Tanh)
 
         offs_l = load_list(offs, "offs_l")
         wa_raw = [sb.tile([P, PACK, HALF], F32, name="wa_raw%d" % a, tag="wa_raw%d" % a) for a in range(2)]
@@ -252,7 +248,7 @@ def tile_picked_tokfdifkind_none_p_kernel(
             picks.append(pick)
         res = sb.tile([P, PACK * H], F32, name="res", tag="z_bf1", align_bytes=64)
         for t in range(PACK):
-            pieces = [slice(0, 384), slice(384, H)] if t == PACK - 1 else [slice(0, H)]
+            pieces = {0: [slice(0, 128), slice(128, H)], PACK - 1: [slice(0, 384), slice(384, H)]}.get(t, [slice(0, H)])
             for cols in pieces:
                 piece = res[:, t * H : (t + 1) * H][:, cols]
                 nc.vector.tensor_tensor(piece, sums[t][:, cols], picks[t][:, cols], ALU.max)

@@ -68,10 +68,10 @@ def tile_picked_tokfdifkind_none_p_kernel(
         wa_raw = [sb.tile([P, PACK, HALF], F32, name="wa_raw%d" % a, tag="wa_raw%d" % a) for a in range(2)]
         nc.sync.dma_start(out=wa_raw[0][:], in_=wa_rows[:, :, half(0)])
         n3_l = load_list(n3, "n3_l")
-        for q in range(4):
+        for r in range(4):
             nc.sync.dma_start(
-                out=xs[32 * q : 32 * q + 4, :].bitcast(I32),
-                in_=x_scales[0, 4 * q : 4 * q + 4, :].bitcast(I32),
+                out=xs[r:P:32, :].bitcast(I32),
+                in_=x_scales[0, r:16:4, :].bitcast(I32),
             )
         xw = sb.tile([P, T], I32, name="xw", align_bytes=64)
         nc.sync.dma_start(out=xw[:], in_=x_words[0].rearrange("p n t -> p (n t)").bitcast(I32))
@@ -79,9 +79,9 @@ def tile_picked_tokfdifkind_none_p_kernel(
 
         gt_sb = [sb.tile([P, 1], F32, name="gt%d" % t) for t in range(PACK)]
         w1_raw = sb.tile([P, PACK, H], F32, name="w1_raw")
+        nc.sync.dma_start(out=tab_win[0][:], in_=dealt(tab, 0))
         nc.sync.dma_start(out=gt_sb[0][:], in_=dealt(gt, 0))
-        for t in range(2):
-            nc.sync.dma_start(out=tab_win[t][:], in_=dealt(tab, t))
+        nc.sync.dma_start(out=tab_win[1][:], in_=dealt(tab, 1))
         n1_l = load_list(n1, "n1_l")
         n2_l = load_list(n2, "n2_l")
         for t in range(1, PACK):

from contextlib import ExitStack

import concourse.mybir as mybir

F32 = mybir.dt.float32
BF16 = mybir.dt.bfloat16
I32 = mybir.dt.int32
U32 = mybir.dt.uint32
U16 = mybir.dt.uint16
U8 = mybir.dt.uint8
FP8X4 = mybir.dt.float8_e4m3fn_x4
ALU = mybir.AluOpType
ACT = mybir.ActivationFunctionType

P = 128
PACK = 4
T = 2048
S = 512
H = 512
HALF = H // 2
LIST_HALF = HALF // 16

FLOPS = 2 * 2 * 512 * 512 * 512


def half(a):
    return slice(a * HALF, (a + 1) * HALF)


def list_half(lst, a):
    return lst[:, a * LIST_HALF : (a + 1) * LIST_HALF]


def interleave(copy, dst, src):
    copy(
        out=dst.rearrange("p (c i j) -> p c j i", i=4, j=PACK),
        in_=src.rearrange("p j (c i) -> p c j i", i=4),
    )


def tile_picked_tokfdifkind_none_p_kernel(
    tc, x_words, x_scales, wa, gt, w1, tab, offs, n1, n2, n3, n4, out
):
    nc = tc.nc
    with ExitStack() as ctx:
        lists = ctx.enter_context(tc.tile_pool(name="lists", bufs=1))
        sb = ctx.enter_context(tc.tile_pool(name="sb", bufs=1))
        ps = ctx.enter_context(tc.psum_pool(name="ps", bufs=1))

        def load_list(src, name):
            lst = lists.tile([P, S // 16], U16, name=name)
            nc.sync.dma_start(lst[:], src)
            return lst

        def dealt(rows, t):
            return rows.rearrange("(q t e) n -> t q e n", t=PACK, e=8)[t]

        wa_rows = wa.rearrange("(p j) n -> p j n", j=PACK)

        xs = sb.tile([P, T], U8, name="xs", align_bytes=64)
        nc.gpsimd.memset(xs[:].bitcast(I32), 0)
        y_win = [sb.tile([P, 2 * H], F32, name="y_win%d" % t) for t in range(PACK)]
        tab_win = [sb.tile([P, H], F32, name="tab_win%d" % t) for t in range(PACK)]
        nc.vector.memset(y_win[0][:, H:], 0.0)
        nc.scalar.activation(out=y_win[1][:, H:], in_=y_win[0][:, H:], func=ACT.Tanh)

        offs_l = load_list(offs, "offs_l")
        wa_raw = [sb.tile([P, PACK, HALF], F32, name="wa_raw%d" % a, tag="wa_raw%d" % a) for a in range(2)]
        nc.sync.dma_start(out=wa_raw[0][:], in_=wa_rows[:, :, half(0)])
        n3_l = load_list(n3, "n3_l")
        for r in range(4):
            nc.sync.dma_start(
                out=xs[r:P:32, :].bitcast(I32),
                in_=x_scales[0, r:16:4, :].bitcast(I32),
            )
        xw = sb.tile([P, T], I32, name="xw", align_bytes=64)
        nc.sync.dma_start(out=xw[:], in_=x_words[0].rearrange("p n t -> p (n t)").bitcast(I32))
        nc.sync.dma_start(out=wa_raw[1][:], in_=wa_rows[:, :, half(1)])

        gt_sb = [sb.tile([P, 1], F32, name="gt%d" % t) for t in range(PACK)]
        w1_raw = sb.tile([P, PACK, H], F32, name="w1_raw")
        nc.sync.dma_start(out=tab_win[0][:], in_=dealt(tab, 0))
        nc.sync.dma_start(out=gt_sb[0][:], in_=dealt(gt, 0))
        nc.sync.dma_start(out=tab_win[1][:], in_=dealt(tab, 1))
        n1_l = load_list(n1, "n1_l")
        n2_l = load_list(n2, "n2_l")
        for t in range(1, PACK):
            nc.sync.dma_start(out=gt_sb[t][:], in_=dealt(gt, t))
        for j in range(PACK):
            nc.sync.dma_start(out=w1_raw[:, j, :], in_=dealt(w1, j))
        for t in range(2, PACK):
            nc.sync.dma_start(out=tab_win[t][:], in_=dealt(tab, t))
        n4_l = load_list(n4, "n4_l")

        xs_g = sb.tile([P, S], U8, name="xs_g", align_bytes=64)
        nc.vector.tensor_copy(out=xs_g[:], in_=xs[:].indirect(offs_l[:]))
        wa_bf = [sb.tile([P, HALF * PACK], BF16, name="wa_bf%d" % a, tag="wa_bf%d" % a, align_bytes=64) for a in range(2)]
        wa_q = [sb.tile([P, HALF], U32, name="wa_q%d" % a, align_bytes=64) for a in range(2)]
        wa_s = [sb.tile([P, HALF], U8, name="wa_s%d" % a, align_bytes=64) for a in range(2)]
        interleave(nc.scalar.copy, wa_bf[0][:], wa_raw[0][:])
        nc.vector.quantize_mx(out=wa_q[0][:].bitcast(FP8X4), scales=wa_s[0][:], in_=wa_bf[0][:])
        xs_d = sb.tile([P, S], U8, name="xs_d", align_bytes=64)
        nc.vector.tensor_copy(
            out=xs_d[:].bitcast(I32).rearrange("p (t q w) -> p t q w", t=PACK, w=2),
            in_=xs_g[:].bitcast(I32).rearrange("p (q t w) -> p t q w", t=PACK, w=2),
        )
        xw_d = sb.tile([P, S], U32, name="xw_d", align_bytes=64)
        nc.vector.tensor_copy(
            out=xw_d[:].rearrange("p (t q e) -> p q t e", t=PACK, e=8),
            in_=xw[:].bitcast(U32).indirect(offs_l[:]),
        )
        h_win = []

        def fetch_tab(t, tag):
            win = sb.tile([P, 2 * H], F32, name="h_win%d" % t, tag=tag, align_bytes=64)
            for a in range(2):
                nc.vector.tensor_copy(out=win[:, H:][:, half(a)], in_=tab_win[t][:].indirect(list_half(n3_l, a)))
            h_win.append(win)

        interleave(nc.scalar.copy, wa_bf[1][:], wa_raw[1][:])
        fetch_tab(0, "h_win0")
        nc.vector.quantize_mx(out=wa_q[1][:].bitcast(FP8X4), scales=wa_s[1][:], in_=wa_bf[1][:])

        def banks(first_tag, name):
            lone = [ps.tile([P, HALF], F32, name="%s0%d" % (name, a), tag="bank%d" % ((first_tag + a) % 8)) for a in range(2)]
            whole = [ps.tile([P, H], F32, name="%s%d" % (name, t), tag="bank%d" % ((first_tag + 1 + t) % 8)) for t in range(1, PACK)]
            return lone, whole

        def part(bk, t, a):
            return bk[0][a][:] if t == 0 else bk[1][t - 1][:, half(a)]

        def tile_cols(t):
            return slice(t * P, (t + 1) * P)

        y_ps = banks(0, "y")
        for a in range(2):
            for t in range(PACK):
                nc.tensor.matmul_mx(
                    out=part(y_ps, t, a),
                    lhsT=xw_d[:, tile_cols(t)].bitcast(FP8X4),
                    lhsT_scale=xs_d[:, tile_cols(t)],
                    rhs=wa_q[a][:].bitcast(FP8X4),
                    rhs_scale=wa_s[a][:],
                    start=True,
                    stop=True,
                )

        fetch_tab(1, "wa_bf1")

        gy_win = [sb.tile([P, 2 * H], F32, name="gy_win%d" % t, tag="wa_raw1" if t == 0 else "gy_win%d" % t) for t in range(PACK)]
        diff = [sb.tile([P, H], F32, name="diff%d" % t) for t in range(PACK)]
        th = [y_win[2][:, H:], y_win[3][:, H:]]
        th.extend(sb.tile([P, H], F32, name="th%d" % t, tag="th%d" % t, align_bytes=64)[:] for t in range(2, PACK))
        prod_whole = sb.tile([P, PACK, H], F32, name="prod_whole")

        def own(t):
            return gy_win[t][:, H:]

        def differ(t):
            if t == 0:
                nc.scalar.copy(out=own(0)[:, half(0)], in_=part(y_ps, 0, 0))
                nc.scalar.copy(out=y_win[0][:, half(0)], in_=own(0)[:, half(0)])
                nc.scalar.activation(out=gy_win[0][:, half(0)], in_=own(0)[:, half(0)], func=ACT.Copy, scale=gt_sb[0][:])
                nc.scalar.copy(out=y_win[0][:, half(1)], in_=part(y_ps, 0, 1))
                nc.scalar.copy(out=own(0)[:, half(1)], in_=part(y_ps, 0, 1))
            else:
                nc.scalar.copy(out=y_win[t][:, :H], in_=y_ps[1][t - 1][:])
                nc.scalar.copy(out=own(t), in_=y_ps[1][t - 1][:])
            nc.vector.tensor_tensor(diff[t][:], y_win[t][:].indirect(n1_l[:]), own(t), ALU.subtract)

        def weigh(t):
            if t == 0:
                nc.scalar.activation(out=gy_win[0][:, half(1)], in_=part(y_ps, 0, 1), func=ACT.Copy, scale=gt_sb[0][:])
            else:
                nc.scalar.activation(out=gy_win[t][:, :H], in_=y_ps[1][t - 1][:], func=ACT.Copy, scale=gt_sb[t][:])
            nc.scalar.activation(out=th[t], in_=diff[t][:], func=ACT.Tanh)
            if t < PACK - 1:
                nc.vector.tensor_tensor(prod_whole[:, t, :], gy_win[t][:].indirect(n2_l[:]), th[t], ALU.mult)
            else:
                for a in range(2):
                    nc.vector.tensor_tensor(prod_whole[:, t, half(a)], gy_win[t][:].indirect(list_half(n2_l, a)), th[t][:, half(a)], ALU.mult)

        differ(0)
        for t in range(PACK):
            if t + 1 < PACK:
                differ(t + 1)
            weigh(t)

        z_bf = [sb.tile([P, HALF * PACK], BF16, name="z_bf%d" % a, tag="z_bf%d" % a, align_bytes=64) for a in range(2)]
        z_q = [sb.tile([P, HALF], U32, name="z_q%d" % a, align_bytes=64) for a in range(2)]
        z_s = [sb.tile([P, HALF], U8, name="z_s%d" % a, align_bytes=64) for a in range(2)]
        w1_q = [sb.tile([P, P], U32, name="w1_q%d" % t, align_bytes=64) for t in range(PACK)]
        w1_s = [sb.tile([P, P], U8, name="w1_s%d" % t, align_bytes=64) for t in range(PACK)]
        w1_bf = [sb.tile([P, P * PACK], BF16, name="w1_bf%d" % t, align_bytes=64) for t in range(PACK)]

        def cast_w1(t):
            nc.scalar.copy(
                out=w1_bf[t][:].rearrange("p (q u i j) -> p q u j i", u=2, i=4, j=PACK),
                in_=w1_raw[:].rearrange("p j (q t u i) -> p t q u j i", t=PACK, u=2, i=4)[:, t],
            )

        def quantize_w1(t):
            nc.vector.quantize_mx(out=w1_q[t][:].bitcast(FP8X4), scales=w1_s[t][:], in_=w1_bf[t][:])

        h_ps = banks(5, "h")

        def second_product(t, a):
            nc.tensor.matmul_mx(
                out=part(h_ps, t, a),
                lhsT=w1_q[t][:].bitcast(FP8X4),
                lhsT_scale=w1_s[t][:],
                rhs=z_q[a][:].bitcast(FP8X4),
                rhs_scale=z_s[a][:],
                start=True,
                stop=True,
            )

        cast_w1(0)
        for a in range(2):
            interleave(nc.scalar.copy, z_bf[a][:], prod_whole[:, :, half(a)])
        cast_w1(1)
        cast_w1(2)
        fetch_tab(2, "th3")
        quantize_w1(0)
        for a in range(2):
            nc.vector.quantize_mx(out=z_q[a][:].bitcast(FP8X4), scales=z_s[a][:], in_=z_bf[a][:])
        fetch_tab(3, "z_bf1")
        quantize_w1(1)
        quantize_w1(2)
        for a in range(2):
            second_product(0, a)
            nc.scalar.copy(out=h_win[0][:, half(a)], in_=part(h_ps, 0, a))

        sums, picks = [], []
        for t in range(PACK):
            if t > 0:
                for a in range(2):
                    second_product(t, a)
                nc.scalar.copy(out=h_win[t][:, :H], in_=h_ps[1][t - 1][:])
            if t == 1:
                cast_w1(3)
                quantize_w1(3)
            total = sb.tile([P, H], F32, name="total%d" % t)
            pick = sb.tile([P, H], F32, name="pick%d" % t)
            nc.vector.tensor_copy(out=pick[:], in_=h_win[t][:].indirect(n4_l[:]))
            nc.gpsimd.tensor_tensor(total[:], h_win[t][:, :H], h_win[t][:, H:], ALU.add)
            sums.append(total)
            picks.append(pick)
        res = sb.tile([P, PACK * H], F32, name="res", tag="z_bf1", align_bytes=64)
        for t in range(PACK):
            pieces = {0: [slice(0, 128), slice(128, H)], PACK - 1: [slice(0, 384), slice(384, H)]}.get(t, [slice(0, H)])
            for cols in pieces:
                piece = res[:, t * H : (t + 1) * H][:, cols]
                nc.vector.tensor_tensor(piece, sums[t][:, cols], picks[t][:, cols], ALU.max)
                nc.sync.dma_start(out=dealt(out, t)[:, :, cols], in_=piece)
